import numpy as np, ml_dtypes
CORES = [65,73,81,89,97,105,113,121]
N = 8
TK, LAY = 128, 3
def setup_inputs(rng):
    return {"x": rng.standard_normal((N, 128, TK), dtype=np.float32).astype(ml_dtypes.bfloat16), "w": (rng.standard_normal((N, 128, LAY * 256), dtype=np.float32) / 16).astype(ml_dtypes.bfloat16)}
def setup_inputs_big(rng):
    d = setup_inputs(rng)
    for k in ("x", "w"): d[k] = (d[k].astype(np.float32) * 1024.0).astype(d[k].dtype)
    return d
def setup_inputs_small(rng):
    d = setup_inputs(rng)
    for k in ("x", "w"): d[k] = (d[k].astype(np.float32) * (1 / 1024.0)).astype(d[k].dtype)
    return d
def setup_inputs_apart(rng):
    d = setup_inputs(rng)
    f = (10.0 ** rng.permutation(np.linspace(-1.5, 1.5, N))).astype(np.float32).reshape(N, 1, 1)
    for k in ("x", "w"): d[k] = (d[k].astype(np.float32) * f).astype(d[k].dtype)
    return d
def reference(x, w):
    X, W = x.astype(np.float64), w.astype(np.float64)
    h = list(X)
    for l in range(LAY):
        h = [np.maximum(W[r][:, 256 * l:256 * l + 128].T @ h[r] + W[r][:, 256 * l + 128:256 * l + 256].T @ h[r ^ (1 << l)], 0.0) for r in range(N)]
    return {"y": np.stack(h).astype(ml_dtypes.bfloat16)}

@@ -1,0 +1,149 @@
+from concourse.bass import DstId, RemoteDMATransfer
+from concourse.mybir import AluOpType
+
+D = 128
+
+SCRATCH = {
+    "xd": ("dram", [D, D], "bfloat16"),
+    "xw": ("sbuf", [D, 3 * D], "bfloat16"),
+    "pxw": ("sbuf", [D, 3 * D], "bfloat16"),
+    "pm": ("sbuf", [D, D], "bfloat16"),
+    "pd": ("sbuf", [D, D], "bfloat16"),
+    "w12": ("sbuf", [D, 4 * D], "bfloat16"),
+    "zero": ("sbuf", [D, D], "float32"),
+    "h1": ("sbuf", [D, 2 * D], "bfloat16"),
+    "h2": ("sbuf", [D, D], "bfloat16"),
+    "p2": ("sbuf", [D, D], "bfloat16"),
+    "yb": ("sbuf", [D, D], "bfloat16"),
+    "psA": ("psum", [D, 512], "float32"),
+    "psB": ("psum", [D, 512], "float32"),
+    "psC": ("psum", [D, 512], "float32"),
+    "psD": ("psum", [D, 512], "float32"),
+}
+SEMAPHORES = ["ld_xd", "ld_x", "ld_w0", "ld_w12", "zero", "arr_r", "arr_m", "arr_d", "arr_xw", "arr_h2", "sent",
+              "mmA", "mmB", "mmC", "mmD", "rA", "rB", "rC", "rD", "stored"]
+
+
+def _count(mask):
+    return bin(mask).count("1")
+
+
+def _relays(T, topo, r):
+    rc = T.cores[r]
+    near, far = T.cores[r ^ 1], T.cores[r ^ 3]
+    cand = [c for c in range(topo.CHIPS * topo.CORES_PER_CHIP)
+            if topo.chip(c) == topo.chip(rc) and T.rank_of(c) is None
+            and topo.may_write(c, near) and topo.may_write(c, far)]
+    same = [c for c in cand if topo.die(c) == topo.die(rc)]
+    other = [c for c in cand if topo.die(c) != topo.die(rc)]
+    return [(same[0], r ^ 1), (other[0], r ^ 3)]
+
+
+def _hop_a_mask(T, topo, r):
+    rc = T.cores[r]
+    m = topo.mask(rc, T.cores[r ^ 2]) & topo.mask(rc, T.cores[r ^ 4])
+    for c, _ in _relays(T, topo, r):
+        m &= topo.mask(rc, c)
+    return m
+
+
+def _relay_program(g, core, T, topo):
+    S = T.sem
+    for r, rc in enumerate(T.cores):
+        if topo.chip(rc) != topo.chip(core):
+            continue
+        for k, (c, dst_rank) in enumerate(_relays(T, topo, r)):
+            if c != core:
+                continue
+            dst = T.cores[dst_rank]
+            rid, pid, _ = topo.addr(dst)
+            m = topo.mask(core, dst)
+            g.wait_ge(S.arr_r, _count(_hop_a_mask(T, topo, r)))
+            g.remote_dma(out_ap=(T.pm[:] if k == 0 else T.pd[:]), in_ap=T.xd[:],
+                         remote_sem=(S.arr_m if k == 0 else S.arr_d), local_sem=S.sent,
+                         pid=pid, routing_id=rid, dma_engine_mask=m)
+            g.wait_ge(S.sent, _count(m))
+
+
+def rank_program(g, core, T, topo):
+    S = T.sem
+    q = T.rank_of(core)
+    if q is None:
+        _relay_program(g, core, T, topo)
+        return
+    te, ve = g.tensor, g.vector
+
+    g.sync.dma_start(T.xd[:], T.x[:]).then_inc(S.ld_xd, 16)
+    g.scalar.dma_start(T.xw[:, D:3 * D], T.w[:, 0:2 * D]).then_inc(S.ld_w0, 16)
+    g.sync.dma_start(T.xw[:, 0:D], T.x[:]).then_inc(S.ld_x, 16)
+    g.scalar.dma_start(T.w12[:], T.w[:, 2 * D:6 * D]).then_inc(S.ld_w12, 16)
+    ve.memset(T.zero[:], 0.0).then_inc(S.zero, 1)
+
+    relays = _relays(T, topo, q)
+    m_a = _hop_a_mask(T, topo, q)
+    ids = []
+    for c, _ in relays:
+        rid, pid, _se = topo.addr(c)
+        ids.append(DstId(rid=rid, pnc=pid))
+    g.wait_ge(S.ld_xd, 16)
+    g.remote_dma_fused([RemoteDMATransfer(dst_ids=ids, dma_engine_mask=m_a, remote_sem=S.arr_r,
+                                          srcs=[T.xd[:]], dsts=[T.xd[:] for _ in ids], alu_op=0)],
+                       local_sem=S.sent)
+    sent = _count(m_a)
+
+    p1 = T.cores[q ^ 2]
+    rid, pid, _se = topo.addr(p1)
+    m1 = topo.mask(core, p1)
+    g.wait_ge(S.ld_x, 16)
+    g.wait_ge(S.ld_w0, 16)
+    g.remote_dma(out_ap=T.pxw[:], in_ap=T.xw[:], remote_sem=S.arr_xw, local_sem=S.sent,
+                 pid=pid, routing_id=rid, dma_engine_mask=m1)
+    sent += _count(m1)
+
+    p2 = T.cores[q ^ 4]
+    rid, pid, _se = topo.addr(p2)
+    m2 = topo.mask(core, p2)
+    g.wait_ge(S.rC, 1)
+    g.remote_dma(out_ap=T.p2[:], in_ap=T.h2[:], remote_sem=S.arr_h2, local_sem=S.sent,
+                 pid=pid, routing_id=rid, dma_engine_mask=m2)
+    sent += _count(m2)
+    g.wait_ge(S.sent, sent)
+
+    n_xw = _count(topo.mask(T.cores[q ^ 2], core))
+    n_h2 = _count(topo.mask(T.cores[q ^ 4], core))
+    n_m = _count(topo.mask(_relays(T, topo, q ^ 1)[0][0], core))
+    n_d = _count(topo.mask(_relays(T, topo, q ^ 3)[1][0], core))
+
+    A, B, C, E = T.psA[:, 0:D], T.psB[:, 0:D], T.psC[:, 0:D], T.psD[:, 0:D]
+    te.wait_ge(S.ld_x, 16)
+    te.wait_ge(S.ld_w0, 16)
+    te.matmul(A, T.xw[:, D:2 * D], T.xw[:, 0:D], start=True, stop=False).then_inc(S.mmA, 1)
+    te.wait_ge(S.arr_xw, n_xw)
+    te.matmul(B, T.pxw[:, D:2 * D], T.pxw[:, 0:D], start=True, stop=False).then_inc(S.mmB, 1)
+    te.wait_ge(S.arr_m, n_m)
+    te.matmul(A, T.xw[:, 2 * D:3 * D], T.pm[:], start=False, stop=True).then_inc(S.mmA, 1)
+    te.wait_ge(S.arr_d, n_d)
+    te.matmul(B, T.pxw[:, 2 * D:3 * D], T.pd[:], start=False, stop=True).then_inc(S.mmB, 1)
+    te.wait_ge(S.ld_w12, 16)
+    te.wait_ge(S.rA, 1)
+    te.matmul(C, T.w12[:, 0:D], T.h1[:, 0:D], start=True, stop=False).then_inc(S.mmC, 1)
+    te.wait_ge(S.rB, 1)
+    te.matmul(C, T.w12[:, D:2 * D], T.h1[:, D:2 * D], start=False, stop=True).then_inc(S.mmC, 1)
+    te.wait_ge(S.rC, 1)
+    te.matmul(E, T.w12[:, 2 * D:3 * D], T.h2[:], start=True, stop=False).then_inc(S.mmD, 1)
+    te.wait_ge(S.arr_h2, n_h2)
+    te.matmul(E, T.w12[:, 3 * D:4 * D], T.p2[:], start=False, stop=True).then_inc(S.mmD, 1)
+
+    ve.wait_ge(S.zero, 1)
+    ve.wait_ge(S.mmA, 2)
+    ve.tensor_tensor(T.h1[:, 0:D], A, T.zero[:], AluOpType.max).then_inc(S.rA, 1)
+    ve.wait_ge(S.mmB, 2)
+    ve.tensor_tensor(T.h1[:, D:2 * D], B, T.zero[:], AluOpType.max).then_inc(S.rB, 1)
+    ve.wait_ge(S.mmC, 2)
+    ve.tensor_tensor(T.h2[:], C, T.zero[:], AluOpType.max).then_inc(S.rC, 1)
+    ve.wait_ge(S.mmD, 2)
+    ve.tensor_tensor(T.yb[:], E, T.zero[:], AluOpType.max).then_inc(S.rD, 1)
+
+    g.sync.wait_ge(S.rD, 1)
+    g.sync.dma_start(T.y[:], T.yb[:]).then_inc(S.stored, 16)
+    g.sync.wait_ge(S.stored, 16)

@@ -1,149 +1,235 @@
 from concourse.bass import DstId, RemoteDMATransfer
-from concourse.mybir import AluOpType
+from concourse.mybir import AluOpType, ActivationFunctionType
 
 D = 128
 
 SCRATCH = {
     "xd": ("dram", [D, D], "bfloat16"),
-    "xw": ("sbuf", [D, 3 * D], "bfloat16"),
-    "pxw": ("sbuf", [D, 3 * D], "bfloat16"),
-    "pm": ("sbuf", [D, D], "bfloat16"),
-    "pd": ("sbuf", [D, D], "bfloat16"),
+    "u1d": ("dram", [D, D], "bfloat16"),
+    "v1d": ("dram", [D, D], "bfloat16"),
+    "xs": ("sbuf", [D, D], "bfloat16"),
+    "uvz": ("sbuf", [D, 3 * D], "bfloat16"),
     "w12": ("sbuf", [D, 4 * D], "bfloat16"),
+    "px1": ("sbuf", [D, D], "bfloat16"),
+    "px3": ("sbuf", [D, D], "bfloat16"),
+    "px5": ("sbuf", [D, D], "bfloat16"),
+    "px7": ("sbuf", [D, D], "bfloat16"),
+    "pz2": ("sbuf", [D, 2 * D], "bfloat16"),
+    "pz4": ("sbuf", [D, 2 * D], "bfloat16"),
+    "pz6": ("sbuf", [D, 2 * D], "bfloat16"),
+    "pu1": ("sbuf", [D, D], "bfloat16"),
+    "pv1": ("sbuf", [D, D], "bfloat16"),
     "zero": ("sbuf", [D, D], "float32"),
-    "h1": ("sbuf", [D, 2 * D], "bfloat16"),
-    "h2": ("sbuf", [D, D], "bfloat16"),
-    "p2": ("sbuf", [D, D], "bfloat16"),
+    "ones": ("sbuf", [D, D], "bfloat16"),
+    "idn": ("sbuf", [D, D], "bfloat16"),
+    "h1a": ("sbuf", [D, D], "bfloat16"),
+    "h1b": ("sbuf", [D, D], "bfloat16"),
+    "h1c": ("sbuf", [D, D], "bfloat16"),
+    "h1d": ("sbuf", [D, D], "bfloat16"),
+    "h2a": ("sbuf", [D, D], "bfloat16"),
+    "h2b": ("sbuf", [D, D], "bfloat16"),
     "yb": ("sbuf", [D, D], "bfloat16"),
+    "psZ": ("psum", [D, 512], "float32"),
     "psA": ("psum", [D, 512], "float32"),
     "psB": ("psum", [D, 512], "float32"),
     "psC": ("psum", [D, 512], "float32"),
     "psD": ("psum", [D, 512], "float32"),
+    "psE": ("psum", [D, 512], "float32"),
+    "psF": ("psum", [D, 512], "float32"),
+    "psG": ("psum", [D, 512], "float32"),
 }
-SEMAPHORES = ["ld_xd", "ld_x", "ld_w0", "ld_w12", "zero", "arr_r", "arr_m", "arr_d", "arr_xw", "arr_h2", "sent",
-              "mmA", "mmB", "mmC", "mmD", "rA", "rB", "rC", "rD", "stored"]
+SEMAPHORES = ["ld_xd", "ld_u1d", "ld_v1d", "ld_x", "ld_uv", "ld_w12", "zero", "ones", "ident",
+              "arr_f", "ax1", "ax3", "ax5", "ax7", "azv", "au1", "av1", "sent",
+              "mmZ", "zc", "mmA", "mmB", "mmC", "mmD", "mmE", "mmF", "mmG",
+              "rA", "rB", "rC", "rD", "rE", "rF", "rG", "stored"]
 
 
 def _count(mask):
     return bin(mask).count("1")
 
 
-def _relays(T, topo, r):
+def _kinds(T, topo, r):
     rc = T.cores[r]
-    near, far = T.cores[r ^ 1], T.cores[r ^ 3]
-    cand = [c for c in range(topo.CHIPS * topo.CORES_PER_CHIP)
-            if topo.chip(c) == topo.chip(rc) and T.rank_of(c) is None
-            and topo.may_write(c, near) and topo.may_write(c, far)]
-    same = [c for c in cand if topo.die(c) == topo.die(rc)]
-    other = [c for c in cand if topo.die(c) != topo.die(rc)]
-    return [(same[0], r ^ 1), (other[0], r ^ 3)]
+    others = [c for c in range(topo.CHIPS * topo.CORES_PER_CHIP)
+              if topo.chip(c) == topo.chip(rc) and T.rank_of(c) is None]
+    port = [c for c in others if topo.may_write(c, T.cores[r ^ 1])]
+    plain = [c for c in others if c not in port]
+    near = lambda cs: [c for c in cs if topo.die(c) == topo.die(rc)]
+    far = lambda cs: [c for c in cs if topo.die(c) != topo.die(rc)]
+    return near(port), far(port), near(plain), far(plain)
 
 
-def _hop_a_mask(T, topo, r):
+def _roles(T, topo, r):
+    near_port, far_port, _near_plain, far_plain = _kinds(T, topo, r)
+    return [(near_port[0], "x", r ^ 1, "px1", "ax1"),
+            (_kinds(T, topo, r ^ 2)[0][1], "x", r ^ 3, "px3", "ax3"),
+            (far_port[0], "x", r ^ 5, "px5", "ax5"),
+            (far_port[1], "x", r ^ 7, "px7", "ax7"),
+            (far_plain[0], "u1", r ^ 4, "pu1", "au1"),
+            (far_plain[1], "v1", r ^ 4, "pv1", "av1")]
+
+
+def _halves(T, topo, r):
     rc = T.cores[r]
-    m = topo.mask(rc, T.cores[r ^ 2]) & topo.mask(rc, T.cores[r ^ 4])
-    for c, _ in _relays(T, topo, r):
-        m &= topo.mask(rc, c)
-    return m
+    full = topo.mask(rc, _kinds(T, topo, r)[0][0])
+    off = topo.mask(rc, T.cores[r ^ 2]) & topo.mask(rc, T.cores[r ^ 4]) & topo.mask(rc, T.cores[r ^ 6])
+    return full & off, full & ~off
 
 
-def _relay_program(g, core, T, topo):
+def _feed_mask(T, topo, r, core, piece):
+    leaving, staying = _halves(T, topo, r)
+    bits = [1 << i for i in range(staying.bit_length()) if staying >> i & 1]
+    half = len(bits) // 2
+    if piece == "u1":
+        return sum(bits[:half])
+    if piece == "v1":
+        return sum(bits[half:])
+    return staying if topo.chip(core) == topo.chip(T.cores[r]) else leaving
+
+
+def _sender(T, topo, q, k, piece):
+    for c, p, d, _b, _s in _roles(T, topo, q ^ k):
+        if p == piece and d == q:
+            return c
+
+
+def _helper_program(g, core, T, topo):
     S = T.sem
-    for r, rc in enumerate(T.cores):
-        if topo.chip(rc) != topo.chip(core):
-            continue
-        for k, (c, dst_rank) in enumerate(_relays(T, topo, r)):
+    for r in range(len(T.cores)):
+        for c, piece, dst_rank, buf, sem in _roles(T, topo, r):
             if c != core:
                 continue
             dst = T.cores[dst_rank]
-            rid, pid, _ = topo.addr(dst)
+            rid, pid, _se = topo.addr(dst)
             m = topo.mask(core, dst)
-            g.wait_ge(S.arr_r, _count(_hop_a_mask(T, topo, r)))
-            g.remote_dma(out_ap=(T.pm[:] if k == 0 else T.pd[:]), in_ap=T.xd[:],
-                         remote_sem=(S.arr_m if k == 0 else S.arr_d), local_sem=S.sent,
+            g.wait_ge(S.arr_f, _count(_feed_mask(T, topo, r, core, piece)))
+            g.remote_dma(out_ap=T[buf][:], in_ap=T.xd[:], remote_sem=S[sem], local_sem=S.sent,
                          pid=pid, routing_id=rid, dma_engine_mask=m)
             g.wait_ge(S.sent, _count(m))
+
+
+def _ids(topo, cores):
+    out = []
+    for c in cores:
+        rid, pid, _se = topo.addr(c)
+        out.append(DstId(rid=rid, pnc=pid))
+    return out
 
 
 def rank_program(g, core, T, topo):
     S = T.sem
     q = T.rank_of(core)
     if q is None:
-        _relay_program(g, core, T, topo)
+        _helper_program(g, core, T, topo)
         return
-    te, ve = g.tensor, g.vector
+    te, ve, sc = g.tensor, g.vector, g.scalar
 
     g.sync.dma_start(T.xd[:], T.x[:]).then_inc(S.ld_xd, 16)
-    g.scalar.dma_start(T.xw[:, D:3 * D], T.w[:, 0:2 * D]).then_inc(S.ld_w0, 16)
-    g.sync.dma_start(T.xw[:, 0:D], T.x[:]).then_inc(S.ld_x, 16)
-    g.scalar.dma_start(T.w12[:], T.w[:, 2 * D:6 * D]).then_inc(S.ld_w12, 16)
+    sc.dma_start(T.xs[:], T.x[:]).then_inc(S.ld_x, 16)
+    g.sync.dma_start(T.uvz[:, 0:2 * D], T.w[:, 0:2 * D]).then_inc(S.ld_uv, 16)
+    sc.dma_start(T.u1d[:], T.w[:, 2 * D:3 * D]).then_inc(S.ld_u1d, 16)
+    g.sync.dma_start(T.v1d[:], T.w[:, 3 * D:4 * D]).then_inc(S.ld_v1d, 16)
+    sc.dma_start(T.w12[:], T.w[:, 2 * D:6 * D]).then_inc(S.ld_w12, 16)
+    ve.memset(T.ones[:], 1.0).then_inc(S.ones, 1)
     ve.memset(T.zero[:], 0.0).then_inc(S.zero, 1)
 
-    relays = _relays(T, topo, q)
-    m_a = _hop_a_mask(T, topo, q)
-    ids = []
-    for c, _ in relays:
-        rid, pid, _se = topo.addr(c)
-        ids.append(DstId(rid=rid, pnc=pid))
+    roles = _roles(T, topo, q)
+    sent = 0
+
+    groups = {}
+    for c, p, _d, _b, _s in roles:
+        if p == "x":
+            groups.setdefault(_feed_mask(T, topo, q, c, p), []).append(c)
     g.wait_ge(S.ld_xd, 16)
-    g.remote_dma_fused([RemoteDMATransfer(dst_ids=ids, dma_engine_mask=m_a, remote_sem=S.arr_r,
-                                          srcs=[T.xd[:]], dsts=[T.xd[:] for _ in ids], alu_op=0)],
+    tr = []
+    for m, cs in groups.items():
+        tr.append(RemoteDMATransfer(dst_ids=_ids(topo, cs), dma_engine_mask=m, remote_sem=S.arr_f,
+                                    srcs=[T.xd[:]], dsts=[T.xd[:] for _ in cs], alu_op=0))
+        sent += _count(m)
+    g.remote_dma_fused(tr, local_sem=S.sent)
+
+    mz = _halves(T, topo, q)[0]
+    g.wait_ge(S.zc, 1)
+    g.remote_dma_fused([RemoteDMATransfer(dst_ids=_ids(topo, [T.cores[q ^ 2], T.cores[q ^ 4], T.cores[q ^ 6]]),
+                                          dma_engine_mask=mz, remote_sem=S.azv, srcs=[T.uvz[:, D:3 * D]],
+                                          dsts=[T.pz2[:], T.pz4[:], T.pz6[:]], alu_op=0)],
                        local_sem=S.sent)
-    sent = _count(m_a)
+    sent += _count(mz)
 
-    p1 = T.cores[q ^ 2]
-    rid, pid, _se = topo.addr(p1)
-    m1 = topo.mask(core, p1)
-    g.wait_ge(S.ld_x, 16)
-    g.wait_ge(S.ld_w0, 16)
-    g.remote_dma(out_ap=T.pxw[:], in_ap=T.xw[:], remote_sem=S.arr_xw, local_sem=S.sent,
-                 pid=pid, routing_id=rid, dma_engine_mask=m1)
-    sent += _count(m1)
+    g.wait_ge(S.ld_u1d, 16)
+    g.wait_ge(S.ld_v1d, 16)
+    tr = []
+    for c, p, _d, _b, _s in roles:
+        if p != "x":
+            m = _feed_mask(T, topo, q, c, p)
+            tr.append(RemoteDMATransfer(dst_ids=_ids(topo, [c]), dma_engine_mask=m, remote_sem=S.arr_f,
+                                        srcs=[(T.u1d[:] if p == "u1" else T.v1d[:])], dsts=[T.xd[:]], alu_op=0))
+            sent += _count(m)
+    g.remote_dma_fused(tr, local_sem=S.sent)
 
-    p2 = T.cores[q ^ 4]
-    rid, pid, _se = topo.addr(p2)
-    m2 = topo.mask(core, p2)
-    g.wait_ge(S.rC, 1)
-    g.remote_dma(out_ap=T.p2[:], in_ap=T.h2[:], remote_sem=S.arr_h2, local_sem=S.sent,
-                 pid=pid, routing_id=rid, dma_engine_mask=m2)
-    sent += _count(m2)
+    g.wait_ge(S.ones, 1)
+    g.affine_select(T.idn[:], T.ones[:], [[-1, D]], AluOpType.is_equal, 0.0, 0, 1).then_inc(S.ident, 1)
     g.wait_ge(S.sent, sent)
 
-    n_xw = _count(topo.mask(T.cores[q ^ 2], core))
-    n_h2 = _count(topo.mask(T.cores[q ^ 4], core))
-    n_m = _count(topo.mask(_relays(T, topo, q ^ 1)[0][0], core))
-    n_d = _count(topo.mask(_relays(T, topo, q ^ 3)[1][0], core))
+    nx = {k: _count(topo.mask(_sender(T, topo, q, k, "x"), core)) for k in (1, 3, 5, 7)}
+    n_u1 = _count(topo.mask(_sender(T, topo, q, 4, "u1"), core))
+    n_v1 = _count(topo.mask(_sender(T, topo, q, 4, "v1"), core))
+    n_zv = sum(_count(_halves(T, topo, q ^ k)[0]) for k in (2, 4, 6))
 
-    A, B, C, E = T.psA[:, 0:D], T.psB[:, 0:D], T.psC[:, 0:D], T.psD[:, 0:D]
+    Z, A, B, C = T.psZ[:, 0:D], T.psA[:, 0:D], T.psB[:, 0:D], T.psC[:, 0:D]
+    E4, E, F, G = T.psD[:, 0:D], T.psE[:, 0:D], T.psF[:, 0:D], T.psG[:, 0:D]
     te.wait_ge(S.ld_x, 16)
-    te.wait_ge(S.ld_w0, 16)
-    te.matmul(A, T.xw[:, D:2 * D], T.xw[:, 0:D], start=True, stop=False).then_inc(S.mmA, 1)
-    te.wait_ge(S.arr_xw, n_xw)
-    te.matmul(B, T.pxw[:, D:2 * D], T.pxw[:, 0:D], start=True, stop=False).then_inc(S.mmB, 1)
-    te.wait_ge(S.arr_m, n_m)
-    te.matmul(A, T.xw[:, 2 * D:3 * D], T.pm[:], start=False, stop=True).then_inc(S.mmA, 1)
-    te.wait_ge(S.arr_d, n_d)
-    te.matmul(B, T.pxw[:, 2 * D:3 * D], T.pd[:], start=False, stop=True).then_inc(S.mmB, 1)
+    te.wait_ge(S.ld_uv, 16)
+    te.matmul(Z, T.uvz[:, 0:D], T.xs[:], start=True, stop=True).then_inc(S.mmZ, 1)
+    te.matmul(A, T.uvz[:, 0:D], T.xs[:], start=True, stop=False).then_inc(S.mmA, 1)
+    te.wait_ge(S.ident, 1)
+    te.wait_ge(S.azv, n_zv)
+    te.matmul(B, T.idn[:], T.pz2[:, D:2 * D], start=True, stop=False).then_inc(S.mmB, 1)
+    te.matmul(C, T.idn[:], T.pz4[:, D:2 * D], start=True, stop=False).then_inc(S.mmC, 1)
+    te.matmul(E4, T.idn[:], T.pz6[:, D:2 * D], start=True, stop=False).then_inc(S.mmD, 1)
+    te.wait_ge(S.ax1, nx[1])
+    te.matmul(A, T.uvz[:, D:2 * D], T.px1[:], start=False, stop=True).then_inc(S.mmA, 1)
+    te.wait_ge(S.ax3, nx[3])
+    te.matmul(B, T.pz2[:, 0:D], T.px3[:], start=False, stop=True).then_inc(S.mmB, 1)
+    te.wait_ge(S.ax5, nx[5])
+    te.matmul(C, T.pz4[:, 0:D], T.px5[:], start=False, stop=True).then_inc(S.mmC, 1)
+    te.wait_ge(S.ax7, nx[7])
+    te.matmul(E4, T.pz6[:, 0:D], T.px7[:], start=False, stop=True).then_inc(S.mmD, 1)
     te.wait_ge(S.ld_w12, 16)
     te.wait_ge(S.rA, 1)
-    te.matmul(C, T.w12[:, 0:D], T.h1[:, 0:D], start=True, stop=False).then_inc(S.mmC, 1)
+    te.matmul(E, T.w12[:, 0:D], T.h1a[:], start=True, stop=False).then_inc(S.mmE, 1)
     te.wait_ge(S.rB, 1)
-    te.matmul(C, T.w12[:, D:2 * D], T.h1[:, D:2 * D], start=False, stop=True).then_inc(S.mmC, 1)
+    te.matmul(E, T.w12[:, D:2 * D], T.h1b[:], start=False, stop=True).then_inc(S.mmE, 1)
+    te.wait_ge(S.au1, n_u1)
     te.wait_ge(S.rC, 1)
-    te.matmul(E, T.w12[:, 2 * D:3 * D], T.h2[:], start=True, stop=False).then_inc(S.mmD, 1)
-    te.wait_ge(S.arr_h2, n_h2)
-    te.matmul(E, T.w12[:, 3 * D:4 * D], T.p2[:], start=False, stop=True).then_inc(S.mmD, 1)
+    te.matmul(F, T.pu1[:], T.h1c[:], start=True, stop=False).then_inc(S.mmF, 1)
+    te.wait_ge(S.av1, n_v1)
+    te.wait_ge(S.rD, 1)
+    te.matmul(F, T.pv1[:], T.h1d[:], start=False, stop=True).then_inc(S.mmF, 1)
+    te.wait_ge(S.rE, 1)
+    te.matmul(G, T.w12[:, 2 * D:3 * D], T.h2a[:], start=True, stop=False).then_inc(S.mmG, 1)
+    te.wait_ge(S.rF, 1)
+    te.matmul(G, T.w12[:, 3 * D:4 * D], T.h2b[:], start=False, stop=True).then_inc(S.mmG, 1)
 
+    ve.wait_ge(S.mmZ, 1)
+    ve.tensor_copy(T.uvz[:, 2 * D:3 * D], Z).then_inc(S.zc, 1)
     ve.wait_ge(S.zero, 1)
     ve.wait_ge(S.mmA, 2)
-    ve.tensor_tensor(T.h1[:, 0:D], A, T.zero[:], AluOpType.max).then_inc(S.rA, 1)
-    ve.wait_ge(S.mmB, 2)
-    ve.tensor_tensor(T.h1[:, D:2 * D], B, T.zero[:], AluOpType.max).then_inc(S.rB, 1)
+    ve.tensor_tensor(T.h1a[:], A, T.zero[:], AluOpType.max).then_inc(S.rA, 1)
     ve.wait_ge(S.mmC, 2)
-    ve.tensor_tensor(T.h2[:], C, T.zero[:], AluOpType.max).then_inc(S.rC, 1)
-    ve.wait_ge(S.mmD, 2)
-    ve.tensor_tensor(T.yb[:], E, T.zero[:], AluOpType.max).then_inc(S.rD, 1)
+    ve.tensor_tensor(T.h1c[:], C, T.zero[:], AluOpType.max).then_inc(S.rC, 1)
+    ve.wait_ge(S.mmE, 2)
+    ve.tensor_tensor(T.h2a[:], E, T.zero[:], AluOpType.max).then_inc(S.rE, 1)
+    ve.wait_ge(S.mmG, 2)
+    ve.tensor_tensor(T.yb[:], G, T.zero[:], AluOpType.max).then_inc(S.rG, 1)
 
-    g.sync.wait_ge(S.rD, 1)
+    sc.wait_ge(S.mmB, 2)
+    sc.activation(T.h1b[:], B, ActivationFunctionType.Relu).then_inc(S.rB, 1)
+    sc.wait_ge(S.mmD, 2)
+    sc.activation(T.h1d[:], E4, ActivationFunctionType.Relu).then_inc(S.rD, 1)
+    sc.wait_ge(S.mmF, 2)
+    sc.activation(T.h2b[:], F, ActivationFunctionType.Relu).then_inc(S.rF, 1)
+
+    g.sync.wait_ge(S.rG, 1)
     g.sync.dma_start(T.y[:], T.yb[:]).then_inc(S.stored, 16)
     g.sync.wait_ge(S.stored, 16)

@@ -39,7 +39,7 @@ SCRATCH = {
     "psG": ("psum", [D, 512], "float32"),
 }
 SEMAPHORES = ["ld_xd", "ld_u1d", "ld_v1d", "ld_x", "ld_uv", "ld_w12", "zero", "ones", "ident",
-              "arr_f", "ax1", "ax3", "ax5", "ax7", "azv", "au1", "av1", "sent",
+              "arr_f", "ax1", "ax3", "ax5", "ax7", "azv", "azh", "au1", "av1", "sent",
               "mmZ", "zc", "mmA", "mmB", "mmC", "mmD", "mmE", "mmF", "mmG",
               "rA", "rB", "rC", "rD", "rE", "rF", "rG", "stored"]
 
@@ -60,11 +60,12 @@ def _kinds(T, topo, r):
 
 
 def _roles(T, topo, r):
-    near_port, far_port, _near_plain, far_plain = _kinds(T, topo, r)
+    near_port, far_port, near_plain, far_plain = _kinds(T, topo, r)
     return [(near_port[0], "x", r ^ 1, "px1", "ax1"),
             (_kinds(T, topo, r ^ 2)[0][1], "x", r ^ 3, "px3", "ax3"),
             (far_port[0], "x", r ^ 5, "px5", "ax5"),
             (far_port[1], "x", r ^ 7, "px7", "ax7"),
+            (near_plain[0], "z", r ^ 6, "pz6", "azh"),
             (far_plain[0], "u1", r ^ 4, "pu1", "au1"),
             (far_plain[1], "v1", r ^ 4, "pv1", "av1")]
 
@@ -93,19 +94,55 @@ def _sender(T, topo, q, k, piece):
             return c
 
 
-def _helper_program(g, core, T, topo):
-    S = T.sem
+def _chip_helpers(T, topo, q):
+    here = topo.chip(T.cores[q])
+    return sorted({c for r in range(len(T.cores)) for c, _p, _d, _b, _s in _roles(T, topo, r) if topo.chip(c) == here})
+
+
+def _job(T, topo, core):
     for r in range(len(T.cores)):
         for c, piece, dst_rank, buf, sem in _roles(T, topo, r):
-            if c != core:
-                continue
-            dst = T.cores[dst_rank]
-            rid, pid, _se = topo.addr(dst)
-            m = topo.mask(core, dst)
-            g.wait_ge(S.arr_f, _count(_feed_mask(T, topo, r, core, piece)))
-            g.remote_dma(out_ap=T[buf][:], in_ap=T.xd[:], remote_sem=S[sem], local_sem=S.sent,
-                         pid=pid, routing_id=rid, dma_engine_mask=m)
-            g.wait_ge(S.sent, _count(m))
+            if c == core:
+                return r, piece, dst_rank, buf, sem
+    return None
+
+
+def _slice(T, topo, q, core):
+    hs = _chip_helpers(T, topo, q)
+    unit = 8
+    units = D // unit
+    lo, extra = units // len(hs), units % len(hs)
+    i = hs.index(core)
+    a = i * lo + min(i, extra)
+    return a * unit, (a + lo + (1 if i < extra else 0)) * unit
+
+
+def _helper_mask(T, topo, core):
+    return topo.mask(core, T.cores[_job(T, topo, core)[2]])
+
+
+def _helper_program(g, core, T, topo):
+    S = T.sem
+    job = _job(T, topo, core)
+    if job is None:
+        return
+    r, piece, dst_rank, buf, sem = job
+    m = _helper_mask(T, topo, core)
+    home = [q for q in range(len(T.cores)) if topo.chip(T.cores[q]) == topo.chip(core)][0]
+    mi = m & topo.mask(core, T.cores[home])
+    a, b = _slice(T, topo, home, core)
+    g.vector.memset(T.ones[:, a:b], 1.0).then_inc(S.ones, 1)
+    g.wait_ge(S.ones, 1)
+    g.affine_select(T.idn[:, a:b], T.ones[:, a:b], [[-1, b - a]], AluOpType.is_equal, 0.0, -a, 1).then_inc(S.ident, 1)
+    g.wait_ge(S.ident, 1)
+    rid, pid, _se = topo.addr(T.cores[home])
+    g.remote_dma(out_ap=T.idn[:, a:b], in_ap=T.idn[:, a:b], remote_sem=S.ident, local_sem=S.sent,
+                 pid=pid, routing_id=rid, dma_engine_mask=mi)
+    rid, pid, _se = topo.addr(T.cores[dst_rank])
+    g.wait_ge(S.arr_f, _count(_feed_mask(T, topo, r, core, piece)))
+    g.remote_dma(out_ap=T[buf][:], in_ap=(T.pz6[:] if piece == "z" else T.xd[:]), remote_sem=S[sem], local_sem=S.sent,
+                 pid=pid, routing_id=rid, dma_engine_mask=m)
+    g.wait_ge(S.sent, _count(mi) + _count(m))
 
 
 def _ids(topo, cores):
@@ -130,7 +167,6 @@ def rank_program(g, core, T, topo):
     sc.dma_start(T.u1d[:], T.w[:, 2 * D:3 * D]).then_inc(S.ld_u1d, 16)
     g.sync.dma_start(T.v1d[:], T.w[:, 3 * D:4 * D]).then_inc(S.ld_v1d, 16)
     sc.dma_start(T.w12[:], T.w[:, 2 * D:6 * D]).then_inc(S.ld_w12, 16)
-    ve.memset(T.ones[:], 1.0).then_inc(S.ones, 1)
     ve.memset(T.zero[:], 0.0).then_inc(S.zero, 1)
 
     roles = _roles(T, topo, q)
@@ -149,32 +185,36 @@ def rank_program(g, core, T, topo):
     g.remote_dma_fused(tr, local_sem=S.sent)
 
     mz = _halves(T, topo, q)[0]
+    zh = [c for c, p, _d, _b, _s in roles if p == "z"][0]
+    mh = _feed_mask(T, topo, q, zh, "z")
     g.wait_ge(S.zc, 1)
-    g.remote_dma_fused([RemoteDMATransfer(dst_ids=_ids(topo, [T.cores[q ^ 2], T.cores[q ^ 4], T.cores[q ^ 6]]),
+    g.remote_dma_fused([RemoteDMATransfer(dst_ids=_ids(topo, [T.cores[q ^ 2], T.cores[q ^ 4]]),
                                           dma_engine_mask=mz, remote_sem=S.azv, srcs=[T.uvz[:, D:3 * D]],
-                                          dsts=[T.pz2[:], T.pz4[:], T.pz6[:]], alu_op=0)],
+                                          dsts=[T.pz2[:], T.pz4[:]], alu_op=0),
+                        RemoteDMATransfer(dst_ids=_ids(topo, [zh]),
+                                          dma_engine_mask=mh, remote_sem=S.arr_f, srcs=[T.uvz[:, D:3 * D]],
+                                          dsts=[T.pz6[:]], alu_op=0)],
                        local_sem=S.sent)
-    sent += _count(mz)
+    sent += _count(mz) + _count(mh)
 
     g.wait_ge(S.ld_u1d, 16)
     g.wait_ge(S.ld_v1d, 16)
     tr = []
     for c, p, _d, _b, _s in roles:
-        if p != "x":
+        if p in ("u1", "v1"):
             m = _feed_mask(T, topo, q, c, p)
             tr.append(RemoteDMATransfer(dst_ids=_ids(topo, [c]), dma_engine_mask=m, remote_sem=S.arr_f,
                                         srcs=[(T.u1d[:] if p == "u1" else T.v1d[:])], dsts=[T.xd[:]], alu_op=0))
             sent += _count(m)
     g.remote_dma_fused(tr, local_sem=S.sent)
-
-    g.wait_ge(S.ones, 1)
-    g.affine_select(T.idn[:], T.ones[:], [[-1, D]], AluOpType.is_equal, 0.0, 0, 1).then_inc(S.ident, 1)
     g.wait_ge(S.sent, sent)
 
     nx = {k: _count(topo.mask(_sender(T, topo, q, k, "x"), core)) for k in (1, 3, 5, 7)}
     n_u1 = _count(topo.mask(_sender(T, topo, q, 4, "u1"), core))
     n_v1 = _count(topo.mask(_sender(T, topo, q, 4, "v1"), core))
-    n_zv = sum(_count(_halves(T, topo, q ^ k)[0]) for k in (2, 4, 6))
+    n_id = sum(_count(_helper_mask(T, topo, c) & topo.mask(c, core)) for c in _chip_helpers(T, topo, q))
+    n_zv = sum(_count(_halves(T, topo, q ^ k)[0]) for k in (2, 4))
+    n_zh = _count(topo.mask(_sender(T, topo, q, 6, "z"), core))
 
     Z, A, B, C = T.psZ[:, 0:D], T.psA[:, 0:D], T.psB[:, 0:D], T.psC[:, 0:D]
     E4, E, F, G = T.psD[:, 0:D], T.psE[:, 0:D], T.psF[:, 0:D], T.psG[:, 0:D]
@@ -182,17 +222,18 @@ def rank_program(g, core, T, topo):
     te.wait_ge(S.ld_uv, 16)
     te.matmul(Z, T.uvz[:, 0:D], T.xs[:], start=True, stop=True).then_inc(S.mmZ, 1)
     te.matmul(A, T.uvz[:, 0:D], T.xs[:], start=True, stop=False).then_inc(S.mmA, 1)
-    te.wait_ge(S.ident, 1)
+    te.wait_ge(S.ident, n_id)
     te.wait_ge(S.azv, n_zv)
     te.matmul(B, T.idn[:], T.pz2[:, D:2 * D], start=True, stop=False).then_inc(S.mmB, 1)
     te.matmul(C, T.idn[:], T.pz4[:, D:2 * D], start=True, stop=False).then_inc(S.mmC, 1)
-    te.matmul(E4, T.idn[:], T.pz6[:, D:2 * D], start=True, stop=False).then_inc(S.mmD, 1)
     te.wait_ge(S.ax1, nx[1])
     te.matmul(A, T.uvz[:, D:2 * D], T.px1[:], start=False, stop=True).then_inc(S.mmA, 1)
     te.wait_ge(S.ax3, nx[3])
     te.matmul(B, T.pz2[:, 0:D], T.px3[:], start=False, stop=True).then_inc(S.mmB, 1)
     te.wait_ge(S.ax5, nx[5])
     te.matmul(C, T.pz4[:, 0:D], T.px5[:], start=False, stop=True).then_inc(S.mmC, 1)
+    te.wait_ge(S.azh, n_zh)
+    te.matmul(E4, T.idn[:], T.pz6[:, D:2 * D], start=True, stop=False).then_inc(S.mmD, 1)
     te.wait_ge(S.ax7, nx[7])
     te.matmul(E4, T.pz6[:, 0:D], T.px7[:], start=False, stop=True).then_inc(S.mmD, 1)
     te.wait_ge(S.ld_w12, 16)

from concourse.bass import DstId, RemoteDMATransfer
from concourse.mybir import AluOpType, ActivationFunctionType

D = 128

SCRATCH = {
    "xd": ("dram", [D, D], "bfloat16"),
    "u1d": ("dram", [D, D], "bfloat16"),
    "v1d": ("dram", [D, D], "bfloat16"),
    "xs": ("sbuf", [D, D], "bfloat16"),
    "uvz": ("sbuf", [D, 3 * D], "bfloat16"),
    "w12": ("sbuf", [D, 4 * D], "bfloat16"),
    "px1": ("sbuf", [D, D], "bfloat16"),
    "px3": ("sbuf", [D, D], "bfloat16"),
    "px5": ("sbuf", [D, D], "bfloat16"),
    "px7": ("sbuf", [D, D], "bfloat16"),
    "pz2": ("sbuf", [D, 2 * D], "bfloat16"),
    "pz4": ("sbuf", [D, 2 * D], "bfloat16"),
    "pz6": ("sbuf", [D, 2 * D], "bfloat16"),
    "pu1": ("sbuf", [D, D], "bfloat16"),
    "pv1": ("sbuf", [D, D], "bfloat16"),
    "zero": ("sbuf", [D, D], "float32"),
    "ones": ("sbuf", [D, D], "bfloat16"),
    "idn": ("sbuf", [D, D], "bfloat16"),
    "h1a": ("sbuf", [D, D], "bfloat16"),
    "h1b": ("sbuf", [D, D], "bfloat16"),
    "h1c": ("sbuf", [D, D], "bfloat16"),
    "h1d": ("sbuf", [D, D], "bfloat16"),
    "h2a": ("sbuf", [D, D], "bfloat16"),
    "h2b": ("sbuf", [D, D], "bfloat16"),
    "yb": ("sbuf", [D, D], "bfloat16"),
    "psZ": ("psum", [D, 512], "float32"),
    "psA": ("psum", [D, 512], "float32"),
    "psB": ("psum", [D, 512], "float32"),
    "psC": ("psum", [D, 512], "float32"),
    "psD": ("psum", [D, 512], "float32"),
    "psE": ("psum", [D, 512], "float32"),
    "psF": ("psum", [D, 512], "float32"),
    "psG": ("psum", [D, 512], "float32"),
}
SEMAPHORES = ["ld_xd", "ld_u1d", "ld_v1d", "ld_x", "ld_uv", "ld_w12", "zero", "ones", "ident",
              "arr_f", "ax1", "ax3", "ax5", "ax7", "azv", "azh", "au1", "av1", "sent",
              "mmZ", "zc", "mmA", "mmB", "mmC", "mmD", "mmE", "mmF", "mmG",
              "rA", "rB", "rC", "rD", "rE", "rF", "rG", "stored"]


def _count(mask):
    return bin(mask).count("1")


def _kinds(T, topo, r):
    rc = T.cores[r]
    others = [c for c in range(topo.CHIPS * topo.CORES_PER_CHIP)
              if topo.chip(c) == topo.chip(rc) and T.rank_of(c) is None]
    port = [c for c in others if topo.may_write(c, T.cores[r ^ 1])]
    plain = [c for c in others if c not in port]
    near = lambda cs: [c for c in cs if topo.die(c) == topo.die(rc)]
    far = lambda cs: [c for c in cs if topo.die(c) != topo.die(rc)]
    return near(port), far(port), near(plain), far(plain)


def _roles(T, topo, r):
    near_port, far_port, near_plain, far_plain = _kinds(T, topo, r)
    return [(near_port[0], "x", r ^ 1, "px1", "ax1"),
            (_kinds(T, topo, r ^ 2)[0][1], "x", r ^ 3, "px3", "ax3"),
            (far_port[0], "x", r ^ 5, "px5", "ax5"),
            (far_port[1], "x", r ^ 7, "px7", "ax7"),
            (near_plain[0], "z", r ^ 6, "pz6", "azh"),
            (far_plain[0], "u1", r ^ 4, "pu1", "au1"),
            (far_plain[1], "v1", r ^ 4, "pv1", "av1")]


def _halves(T, topo, r):
    rc = T.cores[r]
    full = topo.mask(rc, _kinds(T, topo, r)[0][0])
    off = topo.mask(rc, T.cores[r ^ 2]) & topo.mask(rc, T.cores[r ^ 4]) & topo.mask(rc, T.cores[r ^ 6])
    return full & off, full & ~off


def _feed_mask(T, topo, r, core, piece):
    leaving, staying = _halves(T, topo, r)
    bits = [1 << i for i in range(staying.bit_length()) if staying >> i & 1]
    half = len(bits) // 2
    if piece == "u1":
        return sum(bits[:half])
    if piece == "v1":
        return sum(bits[half:])
    return staying if topo.chip(core) == topo.chip(T.cores[r]) else leaving


def _sender(T, topo, q, k, piece):
    for c, p, d, _b, _s in _roles(T, topo, q ^ k):
        if p == piece and d == q:
            return c


def _chip_helpers(T, topo, q):
    here = topo.chip(T.cores[q])
    return sorted({c for r in range(len(T.cores)) for c, _p, _d, _b, _s in _roles(T, topo, r) if topo.chip(c) == here})


def _job(T, topo, core):
    for r in range(len(T.cores)):
        for c, piece, dst_rank, buf, sem in _roles(T, topo, r):
            if c == core:
                return r, piece, dst_rank, buf, sem
    return None


def _slice(T, topo, q, core):
    hs = _chip_helpers(T, topo, q)
    unit = 8
    units = D // unit
    lo, extra = units // len(hs), units % len(hs)
    i = hs.index(core)
    a = i * lo + min(i, extra)
    return a * unit, (a + lo + (1 if i < extra else 0)) * unit


def _helper_mask(T, topo, core):
    return topo.mask(core, T.cores[_job(T, topo, core)[2]])


def _helper_program(g, core, T, topo):
    S = T.sem
    job = _job(T, topo, core)
    if job is None:
        return
    r, piece, dst_rank, buf, sem = job
    m = _helper_mask(T, topo, core)
    home = [q for q in range(len(T.cores)) if topo.chip(T.cores[q]) == topo.chip(core)][0]
    mi = m & topo.mask(core, T.cores[home])
    a, b = _slice(T, topo, home, core)
    g.vector.memset(T.ones[:, a:b], 1.0).then_inc(S.ones, 1)
    g.wait_ge(S.ones, 1)
    g.affine_select(T.idn[:, a:b], T.ones[:, a:b], [[-1, b - a]], AluOpType.is_equal, 0.0, -a, 1).then_inc(S.ident, 1)
    g.wait_ge(S.ident, 1)
    rid, pid, _se = topo.addr(T.cores[home])
    g.remote_dma(out_ap=T.idn[:, a:b], in_ap=T.idn[:, a:b], remote_sem=S.ident, local_sem=S.sent,
                 pid=pid, routing_id=rid, dma_engine_mask=mi)
    rid, pid, _se = topo.addr(T.cores[dst_rank])
    g.wait_ge(S.arr_f, _count(_feed_mask(T, topo, r, core, piece)))
    g.remote_dma(out_ap=T[buf][:], in_ap=(T.pz6[:] if piece == "z" else T.xd[:]), remote_sem=S[sem], local_sem=S.sent,
                 pid=pid, routing_id=rid, dma_engine_mask=m)
    g.wait_ge(S.sent, _count(mi) + _count(m))


def _ids(topo, cores):
    out = []
    for c in cores:
        rid, pid, _se = topo.addr(c)
        out.append(DstId(rid=rid, pnc=pid))
    return out


def rank_program(g, core, T, topo):
    S = T.sem
    q = T.rank_of(core)
    if q is None:
        _helper_program(g, core, T, topo)
        return
    te, ve, sc = g.tensor, g.vector, g.scalar

    g.sync.dma_start(T.xd[:], T.x[:]).then_inc(S.ld_xd, 16)
    sc.dma_start(T.xs[:], T.x[:]).then_inc(S.ld_x, 16)
    g.sync.dma_start(T.uvz[:, 0:2 * D], T.w[:, 0:2 * D]).then_inc(S.ld_uv, 16)
    sc.dma_start(T.u1d[:], T.w[:, 2 * D:3 * D]).then_inc(S.ld_u1d, 16)
    g.sync.dma_start(T.v1d[:], T.w[:, 3 * D:4 * D]).then_inc(S.ld_v1d, 16)
    sc.dma_start(T.w12[:], T.w[:, 2 * D:6 * D]).then_inc(S.ld_w12, 16)
    ve.memset(T.zero[:], 0.0).then_inc(S.zero, 1)

    roles = _roles(T, topo, q)
    sent = 0

    groups = {}
    for c, p, _d, _b, _s in roles:
        if p == "x":
            groups.setdefault(_feed_mask(T, topo, q, c, p), []).append(c)
    g.wait_ge(S.ld_xd, 16)
    tr = []
    for m, cs in groups.items():
        tr.append(RemoteDMATransfer(dst_ids=_ids(topo, cs), dma_engine_mask=m, remote_sem=S.arr_f,
                                    srcs=[T.xd[:]], dsts=[T.xd[:] for _ in cs], alu_op=0))
        sent += _count(m)
    g.remote_dma_fused(tr, local_sem=S.sent)

    mz = _halves(T, topo, q)[0]
    zh = [c for c, p, _d, _b, _s in roles if p == "z"][0]
    mh = _feed_mask(T, topo, q, zh, "z")
    g.wait_ge(S.zc, 1)
    g.remote_dma_fused([RemoteDMATransfer(dst_ids=_ids(topo, [T.cores[q ^ 2], T.cores[q ^ 4]]),
                                          dma_engine_mask=mz, remote_sem=S.azv, srcs=[T.uvz[:, D:3 * D]],
                                          dsts=[T.pz2[:], T.pz4[:]], alu_op=0),
                        RemoteDMATransfer(dst_ids=_ids(topo, [zh]),
                                          dma_engine_mask=mh, remote_sem=S.arr_f, srcs=[T.uvz[:, D:3 * D]],
                                          dsts=[T.pz6[:]], alu_op=0)],
                       local_sem=S.sent)
    sent += _count(mz) + _count(mh)

    g.wait_ge(S.ld_u1d, 16)
    g.wait_ge(S.ld_v1d, 16)
    tr = []
    for c, p, _d, _b, _s in roles:
        if p in ("u1", "v1"):
            m = _feed_mask(T, topo, q, c, p)
            tr.append(RemoteDMATransfer(dst_ids=_ids(topo, [c]), dma_engine_mask=m, remote_sem=S.arr_f,
                                        srcs=[(T.u1d[:] if p == "u1" else T.v1d[:])], dsts=[T.xd[:]], alu_op=0))
            sent += _count(m)
    g.remote_dma_fused(tr, local_sem=S.sent)
    g.wait_ge(S.sent, sent)

    nx = {k: _count(topo.mask(_sender(T, topo, q, k, "x"), core)) for k in (1, 3, 5, 7)}
    n_u1 = _count(topo.mask(_sender(T, topo, q, 4, "u1"), core))
    n_v1 = _count(topo.mask(_sender(T, topo, q, 4, "v1"), core))
    n_id = sum(_count(_helper_mask(T, topo, c) & topo.mask(c, core)) for c in _chip_helpers(T, topo, q))
    n_zv = sum(_count(_halves(T, topo, q ^ k)[0]) for k in (2, 4))
    n_zh = _count(topo.mask(_sender(T, topo, q, 6, "z"), core))

    Z, A, B, C = T.psZ[:, 0:D], T.psA[:, 0:D], T.psB[:, 0:D], T.psC[:, 0:D]
    E4, E, F, G = T.psD[:, 0:D], T.psE[:, 0:D], T.psF[:, 0:D], T.psG[:, 0:D]
    te.wait_ge(S.ld_x, 16)
    te.wait_ge(S.ld_uv, 16)
    te.matmul(Z, T.uvz[:, 0:D], T.xs[:], start=True, stop=True).then_inc(S.mmZ, 1)
    te.matmul(A, T.uvz[:, 0:D], T.xs[:], start=True, stop=False).then_inc(S.mmA, 1)
    te.wait_ge(S.ident, n_id)
    te.wait_ge(S.azv, n_zv)
    te.matmul(B, T.idn[:], T.pz2[:, D:2 * D], start=True, stop=False).then_inc(S.mmB, 1)
    te.matmul(C, T.idn[:], T.pz4[:, D:2 * D], start=True, stop=False).then_inc(S.mmC, 1)
    te.wait_ge(S.ax1, nx[1])
    te.matmul(A, T.uvz[:, D:2 * D], T.px1[:], start=False, stop=True).then_inc(S.mmA, 1)
    te.wait_ge(S.ax3, nx[3])
    te.matmul(B, T.pz2[:, 0:D], T.px3[:], start=False, stop=True).then_inc(S.mmB, 1)
    te.wait_ge(S.ax5, nx[5])
    te.matmul(C, T.pz4[:, 0:D], T.px5[:], start=False, stop=True).then_inc(S.mmC, 1)
    te.wait_ge(S.azh, n_zh)
    te.matmul(E4, T.idn[:], T.pz6[:, D:2 * D], start=True, stop=False).then_inc(S.mmD, 1)
    te.wait_ge(S.ax7, nx[7])
    te.matmul(E4, T.pz6[:, 0:D], T.px7[:], start=False, stop=True).then_inc(S.mmD, 1)
    te.wait_ge(S.ld_w12, 16)
    te.wait_ge(S.rA, 1)
    te.matmul(E, T.w12[:, 0:D], T.h1a[:], start=True, stop=False).then_inc(S.mmE, 1)
    te.wait_ge(S.rB, 1)
    te.matmul(E, T.w12[:, D:2 * D], T.h1b[:], start=False, stop=True).then_inc(S.mmE, 1)
    te.wait_ge(S.au1, n_u1)
    te.wait_ge(S.rC, 1)
    te.matmul(F, T.pu1[:], T.h1c[:], start=True, stop=False).then_inc(S.mmF, 1)
    te.wait_ge(S.av1, n_v1)
    te.wait_ge(S.rD, 1)
    te.matmul(F, T.pv1[:], T.h1d[:], start=False, stop=True).then_inc(S.mmF, 1)
    te.wait_ge(S.rE, 1)
    te.matmul(G, T.w12[:, 2 * D:3 * D], T.h2a[:], start=True, stop=False).then_inc(S.mmG, 1)
    te.wait_ge(S.rF, 1)
    te.matmul(G, T.w12[:, 3 * D:4 * D], T.h2b[:], start=False, stop=True).then_inc(S.mmG, 1)

    ve.wait_ge(S.mmZ, 1)
    ve.tensor_copy(T.uvz[:, 2 * D:3 * D], Z).then_inc(S.zc, 1)
    ve.wait_ge(S.zero, 1)
    ve.wait_ge(S.mmA, 2)
    ve.tensor_tensor(T.h1a[:], A, T.zero[:], AluOpType.max).then_inc(S.rA, 1)
    ve.wait_ge(S.mmC, 2)
    ve.tensor_tensor(T.h1c[:], C, T.zero[:], AluOpType.max).then_inc(S.rC, 1)
    ve.wait_ge(S.mmE, 2)
    ve.tensor_tensor(T.h2a[:], E, T.zero[:], AluOpType.max).then_inc(S.rE, 1)
    ve.wait_ge(S.mmG, 2)
    ve.tensor_tensor(T.yb[:], G, T.zero[:], AluOpType.max).then_inc(S.rG, 1)

    sc.wait_ge(S.mmB, 2)
    sc.activation(T.h1b[:], B, ActivationFunctionType.Relu).then_inc(S.rB, 1)
    sc.wait_ge(S.mmD, 2)
    sc.activation(T.h1d[:], E4, ActivationFunctionType.Relu).then_inc(S.rD, 1)
    sc.wait_ge(S.mmF, 2)
    sc.activation(T.h2b[:], F, ActivationFunctionType.Relu).then_inc(S.rF, 1)

    g.sync.wait_ge(S.rG, 1)
    g.sync.dma_start(T.y[:], T.yb[:]).then_inc(S.stored, 16)
    g.sync.wait_ge(S.stored, 16)
